import numpy as np
import ml_dtypes


def mxq(x, axis, fmt="e4m3"):
    dtype, down = {"e4m3": (ml_dtypes.float8_e4m3fn, 7), "e5m2": (ml_dtypes.float8_e5m2, 14)}[fmt]
    v = np.moveaxis(np.asarray(x, np.float32).astype(ml_dtypes.bfloat16).astype(np.float64), axis, -1)
    blocks = v.reshape(v.shape[:-1] + (-1, 32))
    amax = np.abs(blocks).max(-1, keepdims=True)
    byte = np.maximum(np.where(amax > 0, np.frexp(amax)[1] - 1 + 127, 0) - down, 1)
    scale = np.exp2(byte - 127.0)
    codes = (blocks / scale).astype(np.float32).astype(dtype).astype(np.float64)
    return np.moveaxis((codes * scale).reshape(v.shape), -1, axis)


WIDE = False


def mx_kscale(k):
    if not WIDE:
        return np.ones(k)
    levels = np.array([10, -10, 5, -5, 0])
    if k % 512:
        return np.exp2(np.random.permutation(np.resize(levels, k // 32))).repeat(32)
    a = np.empty((k // 512, 16))
    for p in range(k // 512):
        a[p, :8] = np.random.permutation(np.resize(levels, 8))
        for g in range(8):
            far = levels[np.abs(levels - a[p, g]) >= 10]
            a[p, g + 8] = far[np.random.randint(len(far))]
    return np.exp2(a.ravel()).repeat(32)


def f64(x):
    return np.asarray(x).astype(np.float64)


def striped(idx):
    return np.tile(idx.reshape(-1, 16).T, (8, 1)).astype(np.uint16)


def unstriped(offs):
    return offs[:16].T.reshape(-1).astype(np.int64)


def striped8(idx):
    return np.concatenate([x.reshape(-1, 16).T for x in idx]).astype(np.uint16)


def runs(offs, k):
    lists = np.stack([offs[16 * r : 16 * r + 16].T.reshape(-1) for r in range(8)]).astype(np.int64)
    return lists[np.arange(k) % 512 // 64]


def pack_weight(w):
    k, n = w.shape
    w = f64(np.asarray(w, np.float32).astype(ml_dtypes.bfloat16)).reshape(k // 32, 32, n)
    amax = np.abs(w).max(1)
    byte = np.clip(np.where(amax > 0, np.frexp(amax)[1] - 1 + 127 - 7, 1), 1, 254)
    scaled = (w * np.exp2(127.0 - byte)[:, None, :]).reshape(k, n).astype(np.float32)
    words = np.ascontiguousarray(scaled.reshape(k // 512, 128, 4, n).transpose(0, 1, 3, 2)).astype(ml_dtypes.float8_e4m3fn).view(np.uint8)
    return words, np.ascontiguousarray(byte.astype(np.uint8).reshape(k // 512, 16, n))


def unpack_weight(words, scales):
    g, p, n, _ = words.shape
    vals = np.ascontiguousarray(words).view(ml_dtypes.float8_e4m3fn).astype(np.float64) * np.repeat(np.exp2(scales.astype(np.float64) - 127.0), 8, axis=1)[..., None]
    return vals.transpose(0, 1, 3, 2).reshape(g * 512, n)


E2M1 = np.array([0.0, 0.5, 1.0, 1.5, 2.0, 3.0, 4.0, 6.0, -0.0, -0.5, -1.0, -1.5, -2.0, -3.0, -4.0, -6.0])


def pack_fp4(w):
    k, n = w.shape
    w = f64(np.asarray(w, np.float32).astype(ml_dtypes.bfloat16)).reshape(k // 32, 32, n)
    amax = np.abs(w).max(1)
    mant, ex = np.frexp(amax / 6.0)
    byte = np.clip(np.where(amax > 0, np.where(mant > 0.5, ex, ex - 1) + 127, 1), 1, 254)
    scaled = (w * np.exp2(127.0 - byte)[:, None, :]).reshape(k, n).astype(np.float32)
    c = np.ascontiguousarray(scaled.reshape(k // 512, 128, 4, n).transpose(0, 1, 3, 2)).astype(ml_dtypes.float4_e2m1fn).view(np.uint8) & 0xF
    words = (c[..., 0::2] | (c[..., 1::2] << 4)).reshape(k // 512, 128, 2 * n)
    return np.ascontiguousarray(words), np.ascontiguousarray(byte.astype(np.uint8).reshape(k // 512, 16, n))


def unpack_fp4(words, scales):
    g, _, n = scales.shape
    words = np.ascontiguousarray(words).reshape(g, 128, n, 2)
    nib = np.empty((g, 128, n, 4), np.uint8)
    nib[..., 0::2] = words & 0xF
    nib[..., 1::2] = words >> 4
    vals = E2M1[nib] * np.repeat(np.exp2(scales.astype(np.float64) - 127.0), 8, axis=1)[..., None]
    return vals.transpose(0, 1, 3, 2).reshape(g * 512, n)


def sigmoid(v):
    return 1.0 / (1.0 + np.exp(-np.maximum(v, -700.0)))

def planes(y):
    n, m = y.shape
    v = y.astype(np.float32).astype(ml_dtypes.bfloat16).astype(np.float64).reshape(n // 32, 32, m)
    top = np.abs(v).max(1)
    byte = np.clip(np.where(top > 0, np.frexp(top)[1] - 1 + 127 - 7, 1), 1, 254)
    codes = (v * np.exp2(127.0 - byte)[:, None, :]).reshape(n, m).astype(np.float32).astype(ml_dtypes.float8_e4m3fn).view(np.uint8)
    words = codes.reshape(n // 512, 128, 4, m).transpose(0, 1, 3, 2)
    return np.ascontiguousarray(words), np.ascontiguousarray(byte.astype(np.uint8).reshape(n // 512, 16, m))


K, T, S, N, H, G, W = 512, 2048, 512, 512, 512, 2048, 384


def setup_inputs():
    n = np.random.standard_normal
    s = mx_kscale(K)[:, None]
    u = mx_kscale(S)
    packed_xT = pack_weight(n((K, T)) * s)
    packed_w1 = pack_fp4(n((K, H)) / np.sqrt(K) / s)
    packed_dT = pack_weight(n((K, G)) / s)
    packed_w2 = pack_fp4(n((H, N)) / np.sqrt(H) / u[:, None])
    return {
        "x_words": packed_xT[0],
        "x_scales": packed_xT[1],
        "w1_words": packed_w1[0],
        "w1_scales": packed_w1[1],
        "d_words": packed_dT[0],
        "d_scales": packed_dT[1],
        "gn": (np.random.uniform(0.5, 1.5, (H, 1)) * u[:, None]).astype(np.float32),
        "w2_words": packed_w2[0],
        "w2_scales": packed_w2[1],
        "offs": striped(np.random.permutation(T)[:S]),
        "k1": striped8(np.random.randint(0, G, (8, H))),
        "two": striped(np.random.permutation(T)[:S]),
        "n1": striped8(np.stack([np.random.permutation(S) for _ in range(8)])),
        "n2": striped8(np.stack([np.random.permutation(S) for _ in range(8)])),
        "n3": striped(np.random.permutation(S)[:W]),
        "n4": striped(np.random.permutation(S)[:W]),
    }


def reference(x_words, x_scales, w1_words, w1_scales, d_words, d_scales, gn, w2_words, w2_scales, offs, k1, two, n1, n2, n3, n4):
    xq = unpack_weight(x_words, x_scales)[:, unstriped(offs)]
    y = unpack_fp4(w1_words, w1_scales).T @ xq
    d_k1 = unpack_weight(d_words, d_scales)[np.arange(K)[:, None], runs(k1, K)]
    x_two = unpack_weight(x_words, x_scales)[:, unstriped(two)]
    d = 0.0625 * (d_k1.T @ x_two)
    z = f64(gn) * (y + (sigmoid(d[np.arange(H)[:, None], runs(n2, H)] - d)) * (y[np.arange(H)[:, None], runs(n1, H)] - y))
    h = unpack_fp4(w2_words, w2_scales).T @ mxq(z, 0, "e4m3")
    old = h[:, unstriped(n3)]
    pa = h[:, unstriped(n4)]
    ra = old * sigmoid(pa)
    out = h.copy()
    out[:, unstriped(n3)] = ra
    return (out,) + planes(out)

@@ -1,0 +1,236 @@
+from contextlib import ExitStack
+
+import concourse.mybir as mybir
+
+F32 = mybir.dt.float32
+BF16 = mybir.dt.bfloat16
+I32 = mybir.dt.int32
+U32 = mybir.dt.uint32
+U16 = mybir.dt.uint16
+U8 = mybir.dt.uint8
+FP8X4 = mybir.dt.float8_e4m3fn_x4
+FP4X4 = mybir.dt.float4_e2m1fn_x4
+ACT = mybir.ActivationFunctionType
+ALU = mybir.AluOpType
+
+P = 128
+PACK = 4
+T = 2048
+S = 512
+W = 384
+HALF = S // 2
+RING = 3
+FLOPS = 3 * 2 * 512 * 512 * 512
+
+
+def tile_picked_twkeypullbkgate_none_po_kernel(
+    tc, x_words, x_scales, w1_words, w1_scales, d_words, d_scales, gn, w2_words, w2_scales,
+    offs, k1, two, n1, n2, n3, n4, out_0, out_1, out_2,
+):
+    nc = tc.nc
+    with ExitStack() as ctx:
+        keep = ctx.enter_context(tc.tile_pool(name="keep", bufs=1))
+        psum = ctx.enter_context(tc.psum_pool(name="psum", bufs=1))
+
+        def sb(name, shape, dtype, tag=None):
+            return keep.tile(shape, dtype, name=name, tag=tag or name, align_bytes=64)
+
+        def load_list(name, src):
+            tile = sb(name, list(src.shape), U16)
+            nc.sync.dma_start(tile[:], src)
+            return tile
+
+        def load_scale_rows(queue, plane, scales):
+            for q in range(4):
+                queue.dma_start(plane[32 * q : 32 * q + 4, :].bitcast(I32), scales[0, 4 * q : 4 * q + 4, :].bitcast(I32))
+
+        def words_view(ap):
+            return ap[0].rearrange("p n t -> p (n t)").bitcast(I32)
+
+        x_plane = sb("x_plane", [P, T], U8)
+        d_plane = sb("d_plane", [P, T], U8)
+        w1_plane = sb("w1_plane", [P, S], U8)
+        w2_plane = sb("w2_plane", [P, S], U8)
+        dk_plane = sb("dk_plane", [P, S], U8)
+        nc.vector.memset(x_plane[:].bitcast(I32), 0)
+        nc.vector.memset(w1_plane[:].bitcast(I32), 0)
+        nc.gpsimd.memset(d_plane[:].bitcast(I32), 0)
+        nc.gpsimd.memset(w2_plane[:].bitcast(I32), 0)
+        nc.gpsimd.memset(dk_plane[:].bitcast(I32), 0)
+
+        offs_t = load_list("offs_t", offs)
+        load_scale_rows(nc.sync, x_plane, x_scales)
+        x_tab = sb("x_tab", [P, T], U32)
+        nc.sync.dma_start(x_tab[:].bitcast(I32), words_view(x_words))
+        w1_raw = sb("w1_raw", [P, 2 * S], U8)
+        nc.sync.dma_start(w1_raw[:].bitcast(I32), w1_words[0].bitcast(I32))
+        load_scale_rows(nc.sync, w1_plane, w1_scales)
+        for a in range(2):
+            nc.gpsimd.dma_start(d_plane[a:P:16, :].bitcast(I32), d_scales[0, a:16:2, :].bitcast(I32))
+        d_tab = sb("d_tab", [P, T], U32)
+        nc.sync.dma_start(d_tab[:].bitcast(I32), words_view(d_words))
+        k1_t = load_list("k1_t", k1)
+        two_t = load_list("two_t", two)
+        gain = sb("gain", [P, PACK], F32)
+        nc.gpsimd.dma_start(gain[:], gn.rearrange("(p t) o -> p (t o)", t=PACK))
+        n1_t = load_list("n1_t", n1)
+        n2_t = load_list("n2_t", n2)
+        w2_raw = sb("w2_raw", [P, 2 * S], U8)
+        nc.sync.dma_start(w2_raw[:].bitcast(I32), w2_words[0].bitcast(I32))
+        load_scale_rows(nc.gpsimd, w2_plane, w2_scales)
+        n3_t = load_list("n3_t", n3)
+        n4_t = load_list("n4_t", n4)
+
+        def deal(engine_copy, dst, src):
+            engine_copy(dst.rearrange("p (t m) -> p t m", t=PACK), src.rearrange("p (m t) -> p t m", t=PACK))
+
+        def gather_packed(name, window, offsets, dtype):
+            picked = sb(name, [P, S], dtype)
+            nc.vector.tensor_copy(picked[:], window[:].indirect(offsets[:]))
+            return picked
+
+        xo_scale = gather_packed("xo_scale", x_plane, offs_t, U8)
+        w1_code = sb("w1_code", [P, 2 * S], U8)
+        w1_scale = sb("w1_scale", [P, S], U8)
+        deal(nc.scalar.copy, w1_code[:].bitcast(U16), w1_raw[:].bitcast(U16))
+        deal(nc.vector.tensor_copy, w1_scale[:], w1_plane[:])
+
+        xo_code = gather_packed("xo_code", x_tab, offs_t, U32)
+
+        dk_bytes = gather_packed("dk_bytes", d_plane, k1_t, U8)
+        dk_dealt = sb("dk_dealt", [P, S], U8)
+        deal(nc.vector.tensor_copy, dk_dealt[:], dk_bytes[:])
+        for a in range(4):
+            src_row = 16 * (a // 2) + a % 2
+            nc.sync.dma_start(dk_plane[a:P:32, :].bitcast(I32), dk_dealt[src_row:P:32, :].bitcast(I32))
+
+        def product(bank, cols, lhs, lhs_scale, rhs, rhs_scale):
+            nc.tensor.matmul_mx(out=bank[:, cols], lhsT=lhs, lhsT_scale=lhs_scale, rhs=rhs.bitcast(FP8X4), rhs_scale=rhs_scale, start=True, stop=True)
+
+        def fp4_slice(code, t):
+            return code[:, 2 * P * t : 2 * P * (t + 1)].bitcast(FP4X4)
+
+        whole = slice(0, S)
+        halves = [slice(HALF * h, HALF * (h + 1)) for h in range(2)]
+        lcols = [slice(HALF // 16 * h, HALF // 16 * (h + 1)) for h in range(2)]
+
+        y_win = []
+        for t in range(PACK):
+            bank = psum.tile([P, S], F32, name=f"y_bank{t}", tag=f"bank{t}")
+            product(bank, whole, fp4_slice(w1_code, t), w1_scale[:, P * t : P * (t + 1)], xo_code[:], xo_scale[:])
+            win = sb(f"y_win{t}", [P, S], F32)
+            nc.scalar.activation(win[:], bank[:], ACT.Copy, scale=gain[:, t : t + 1])
+            y_win.append(win)
+
+        def fetch(name, window, offsets, tag=None):
+            got = sb(name, [P, HALF], F32, tag)
+            nc.scalar.activation(got[:], window[:].indirect(offsets), ACT.Copy)
+            return got
+
+        y_got = []
+        for t in range(PACK):
+            got = sb(f"y_got{t}", [P, S], F32)
+            for h in range(2):
+                nc.scalar.activation(got[:, halves[h]], y_win[t][:].indirect(n1_t[:, lcols[h]]), ACT.Copy)
+            y_got.append(got)
+
+        xt_scale = gather_packed("xt_scale", x_plane, two_t, U8)
+        xt_code = gather_packed("xt_code", x_tab, two_t, U32)
+        dk_words = gather_packed("dk_words", d_tab, k1_t, U32)
+        dk_code = sb("dk_code", [P, S], U32)
+        deal(nc.vector.tensor_copy, dk_code[:], dk_words[:])
+
+        w2_code = sb("w2_code", [P, 2 * S], U8)
+        w2_scale = sb("w2_scale", [P, S], U8)
+        deal(nc.scalar.copy, w2_code[:].bitcast(U16), w2_raw[:].bitcast(U16))
+        deal(nc.gpsimd.tensor_copy, w2_scale[:], w2_plane[:])
+
+        d_win = []
+        for t in range(PACK):
+            bank = psum.tile([P, S], F32, name=f"d_bank{t}", tag=f"bank{PACK + t}")
+            product(bank, whole, dk_code[:, P * t : P * (t + 1)].bitcast(FP8X4), dk_plane[:, P * t : P * (t + 1)], xt_code[:], xt_scale[:])
+            win = sb(f"d_win{t}", [P, S], F32)
+            nc.scalar.copy(win[:], bank[:])
+            d_win.append(win)
+
+        pull = []
+        for t in range(PACK):
+            diff = sb(f"pull{t}", [P, S], F32)
+            nc.vector.tensor_tensor(diff[:], y_got[t][:], y_win[t][:], ALU.subtract)
+            pull.append(diff)
+
+        h_bank = [psum.tile([P, S], F32, name=f"h_bank{t}", tag=f"bank{t}") for t in range(PACK)]
+        h_win = [sb(f"h_win{t}", [P, S], F32) for t in range(PACK)]
+        g_win = [sb(f"g_win{t}", [P, S], F32) for t in range(PACK)]
+
+        def interleave(dst, planes):
+            nc.vector.tensor_copy(
+                dst.rearrange("p (c i t) -> p c t i", i=4, t=PACK),
+                planes.rearrange("p t (c i) -> p c t i", i=4),
+            )
+
+        ring = []
+
+        def ring_tag():
+            ring.append(len(ring))
+            return f"ring{ring[-1] % RING}"
+
+        def empty_h(h):
+            for t in range(PACK):
+                nc.vector.tensor_copy(h_win[t][:, halves[h]], h_bank[t][:, halves[h]])
+                nc.scalar.activation(g_win[t][:, halves[h]], h_bank[t][:, halves[h]], ACT.Tanh, scale=0.5)
+
+        for h in range(2):
+            cols = halves[h]
+            if h == 1:
+                empty_h(0)
+            z_planes = sb(f"z_planes{h}", [P, PACK, HALF], BF16)
+            gate = []
+            for t in range(PACK + 1):
+                if t < PACK:
+                    d_got = fetch(f"d_got{h}{t}", d_win[t], n2_t[:, lcols[h]], ring_tag())
+                    gap = sb(f"gap{h}{t}", [P, HALF], F32)
+                    nc.vector.tensor_tensor(gap[:], d_got[:], d_win[t][:, cols], ALU.subtract)
+                if t > 0:
+                    u = t - 1
+                    step = sb(f"step{h}{u}", [P, HALF], F32)
+                    nc.vector.scalar_tensor_tensor(step[:], gate[u][:], 1.0, pull[u][:, cols], ALU.add, ALU.mult)
+                    nc.vector.scalar_tensor_tensor(z_planes[:, u, :], step[:], 0.5, y_win[u][:, cols], ALU.mult, ALU.add)
+                if t < PACK:
+                    gate.append(sb(f"gate{h}{t}", [P, HALF], F32))
+                    nc.scalar.activation(gate[t][:], gap[:], ACT.Tanh, scale=0.03125)
+            z_grouped = sb(f"z_grouped{h}", [P, PACK * HALF], BF16)
+            interleave(z_grouped[:], z_planes[:])
+            z_code = sb(f"z_code{h}", [P, HALF], U32)
+            z_scale = sb(f"z_scale{h}", [P, HALF], U8)
+            nc.vector.quantize_mx(out=z_code[:].bitcast(FP8X4), scales=z_scale[:], in_=z_grouped[:])
+            for t in range(PACK):
+                product(h_bank[t], cols, fp4_slice(w2_code, t), w2_scale[:, P * t : P * (t + 1)], z_code[:], z_scale[:])
+        empty_h(1)
+
+        out_rows = out_0.rearrange("(p t) c -> p t c", t=PACK)
+        o_grouped = [sb(f"o_grouped{h}", [P, PACK * HALF], BF16) for h in range(2)]
+        new = []
+        for t in range(PACK + 1):
+            if t < PACK:
+                old = sb(f"old{t}", [P, W], F32)
+                nc.scalar.activation(old[:], h_win[t][:].indirect(n3_t[:]), ACT.Copy, scale=0.5)
+                g_got = sb(f"g_got{t}", [P, W], F32)
+                nc.vector.tensor_copy(g_got[:], g_win[t][:].indirect(n4_t[:]))
+                ra = sb(f"ra{t}", [P, W], F32)
+                nc.vector.scalar_tensor_tensor(ra[:], g_got[:], 1.0, old[:], ALU.add, ALU.mult)
+                new.append(ra)
+            if t > 0:
+                u = t - 1
+                nc.scalar.activation(h_win[u][:].indirect(n3_t[:]), new[u][:], ACT.Copy)
+                nc.sync.dma_start(out_rows[:, u, :], h_win[u][:])
+                for h in range(2):
+                    nc.vector.tensor_copy(o_grouped[h][:, u : PACK * HALF : PACK], h_win[u][:, halves[h]])
+
+        o_code = sb("o_code", [P, S], U32)
+        o_scale = sb("o_scale", [P, S], U8)
+        for h in range(2):
+            nc.vector.quantize_mx(out=o_code[:, halves[h]].bitcast(FP8X4), scales=o_scale[:, halves[h]], in_=o_grouped[h][:])
+            nc.sync.dma_start(words_view(out_1)[:, halves[h]], o_code[:, halves[h]].bitcast(I32))
+        for q in range(4):
+            nc.scalar.dma_start(out_2[0, 4 * q : 4 * q + 4, :].bitcast(I32), o_scale[32 * q : 32 * q + 4, :].bitcast(I32))

@@ -20,6 +20,7 @@ S = 512
 W = 384
 HALF = S // 2
 RING = 3
+V_EMPTIES = 3
 FLOPS = 3 * 2 * 512 * 512 * 512
 
 
@@ -49,34 +50,34 @@ def tile_picked_twkeypullbkgate_none_po_kernel(
 
         x_plane = sb("x_plane", [P, T], U8)
         d_plane = sb("d_plane", [P, T], U8)
-        w1_plane = sb("w1_plane", [P, S], U8)
+        w1_plane = sb("w1_plane", [P, S], U8, "relay")
         w2_plane = sb("w2_plane", [P, S], U8)
         dk_plane = sb("dk_plane", [P, S], U8)
         nc.vector.memset(x_plane[:].bitcast(I32), 0)
         nc.vector.memset(w1_plane[:].bitcast(I32), 0)
-        nc.gpsimd.memset(d_plane[:].bitcast(I32), 0)
-        nc.gpsimd.memset(w2_plane[:].bitcast(I32), 0)
-        nc.gpsimd.memset(dk_plane[:].bitcast(I32), 0)
+        nc.vector.memset(d_plane[:].bitcast(I32), 0)
+        nc.vector.memset(w2_plane[:].bitcast(I32), 0)
+        nc.vector.memset(dk_plane[:].bitcast(I32), 0)
 
         offs_t = load_list("offs_t", offs)
-        load_scale_rows(nc.sync, x_plane, x_scales)
-        x_tab = sb("x_tab", [P, T], U32)
-        nc.sync.dma_start(x_tab[:].bitcast(I32), words_view(x_words))
         w1_raw = sb("w1_raw", [P, 2 * S], U8)
         nc.sync.dma_start(w1_raw[:].bitcast(I32), w1_words[0].bitcast(I32))
+        load_scale_rows(nc.sync, x_plane, x_scales)
+        two_t = load_list("two_t", two)
+        x_tab = sb("x_tab", [P, T], U32)
+        nc.sync.dma_start(x_tab[:].bitcast(I32), words_view(x_words))
         load_scale_rows(nc.sync, w1_plane, w1_scales)
+        w2_raw = sb("w2_raw", [P, 2 * S], U8)
+        nc.gpsimd.dma_start(w2_raw[:].bitcast(I32), w2_words[0].bitcast(I32))
         for a in range(2):
             nc.gpsimd.dma_start(d_plane[a:P:16, :].bitcast(I32), d_scales[0, a:16:2, :].bitcast(I32))
+        k1_t = load_list("k1_t", k1)
+        gain = sb("gain", [P, PACK], F32)
+        nc.sync.dma_start(gain[:], gn.rearrange("(p t) o -> p (t o)", t=PACK))
         d_tab = sb("d_tab", [P, T], U32)
         nc.sync.dma_start(d_tab[:].bitcast(I32), words_view(d_words))
-        k1_t = load_list("k1_t", k1)
-        two_t = load_list("two_t", two)
-        gain = sb("gain", [P, PACK], F32)
-        nc.gpsimd.dma_start(gain[:], gn.rearrange("(p t) o -> p (t o)", t=PACK))
         n1_t = load_list("n1_t", n1)
         n2_t = load_list("n2_t", n2)
-        w2_raw = sb("w2_raw", [P, 2 * S], U8)
-        nc.sync.dma_start(w2_raw[:].bitcast(I32), w2_words[0].bitcast(I32))
         load_scale_rows(nc.gpsimd, w2_plane, w2_scales)
         n3_t = load_list("n3_t", n3)
         n4_t = load_list("n4_t", n4)
@@ -84,20 +85,20 @@ def tile_picked_twkeypullbkgate_none_po_kernel(
         def deal(engine_copy, dst, src):
             engine_copy(dst.rearrange("p (t m) -> p t m", t=PACK), src.rearrange("p (m t) -> p t m", t=PACK))
 
-        def gather_packed(name, window, offsets, dtype):
-            picked = sb(name, [P, S], dtype)
+        def gather_packed(name, window, offsets, dtype, tag=None):
+            picked = sb(name, [P, S], dtype, tag)
             nc.vector.tensor_copy(picked[:], window[:].indirect(offsets[:]))
             return picked
 
         xo_scale = gather_packed("xo_scale", x_plane, offs_t, U8)
+        xt_scale = gather_packed("xt_scale", x_plane, two_t, U8)
+        xo_code = gather_packed("xo_code", x_tab, offs_t, U32)
         w1_code = sb("w1_code", [P, 2 * S], U8)
         w1_scale = sb("w1_scale", [P, S], U8)
         deal(nc.scalar.copy, w1_code[:].bitcast(U16), w1_raw[:].bitcast(U16))
         deal(nc.vector.tensor_copy, w1_scale[:], w1_plane[:])
 
-        xo_code = gather_packed("xo_code", x_tab, offs_t, U32)
-
-        dk_bytes = gather_packed("dk_bytes", d_plane, k1_t, U8)
+        dk_bytes = gather_packed("dk_bytes", d_plane, k1_t, U8, "relay")
         dk_dealt = sb("dk_dealt", [P, S], U8)
         deal(nc.vector.tensor_copy, dk_dealt[:], dk_bytes[:])
         for a in range(4):
@@ -127,6 +128,7 @@ def tile_picked_twkeypullbkgate_none_po_kernel(
             nc.scalar.activation(got[:], window[:].indirect(offsets), ACT.Copy)
             return got
 
+        last = PACK - 1
         y_got = []
         for t in range(PACK):
             got = sb(f"y_got{t}", [P, S], F32)
@@ -134,98 +136,103 @@ def tile_picked_twkeypullbkgate_none_po_kernel(
                 nc.scalar.activation(got[:, halves[h]], y_win[t][:].indirect(n1_t[:, lcols[h]]), ACT.Copy)
             y_got.append(got)
 
-        xt_scale = gather_packed("xt_scale", x_plane, two_t, U8)
-        xt_code = gather_packed("xt_code", x_tab, two_t, U32)
+        xt_code = gather_packed("xt_code", x_tab, two_t, U32, "relay")
         dk_words = gather_packed("dk_words", d_tab, k1_t, U32)
         dk_code = sb("dk_code", [P, S], U32)
-        deal(nc.vector.tensor_copy, dk_code[:], dk_words[:])
+        nc.vector.tensor_copy(dk_code[:].rearrange("p (t m) -> p m t", t=PACK), dk_words[:].rearrange("p (m t) -> p m t", t=PACK))
 
         w2_code = sb("w2_code", [P, 2 * S], U8)
         w2_scale = sb("w2_scale", [P, S], U8)
         deal(nc.scalar.copy, w2_code[:].bitcast(U16), w2_raw[:].bitcast(U16))
         deal(nc.gpsimd.tensor_copy, w2_scale[:], w2_plane[:])
 
-        d_win = []
+        d_bank = []
         for t in range(PACK):
-            bank = psum.tile([P, S], F32, name=f"d_bank{t}", tag=f"bank{PACK + t}")
-            product(bank, whole, dk_code[:, P * t : P * (t + 1)].bitcast(FP8X4), dk_plane[:, P * t : P * (t + 1)], xt_code[:], xt_scale[:])
-            win = sb(f"d_win{t}", [P, S], F32)
-            nc.scalar.copy(win[:], bank[:])
-            d_win.append(win)
+            d_bank.append(psum.tile([P, S], F32, name=f"d_bank{t}", tag=f"bank{PACK + t}"))
+            product(d_bank[t], whole, dk_code[:, P * t : P * (t + 1)].bitcast(FP8X4), dk_plane[:, P * t : P * (t + 1)], xt_code[:], xt_scale[:])
+        d_win = [sb(f"d_win{t}", [P, S], F32) for t in range(V_EMPTIES)]
+        h_bank = [psum.tile([P, S], F32, name=f"h_bank{t}", tag=f"bank{t}") for t in range(PACK)]
 
         pull = []
         for t in range(PACK):
-            diff = sb(f"pull{t}", [P, S], F32)
-            nc.vector.tensor_tensor(diff[:], y_got[t][:], y_win[t][:], ALU.subtract)
-            pull.append(diff)
+            if t < V_EMPTIES:
+                nc.vector.tensor_copy(d_win[t][:], d_bank[t][:])
+            pull.append(sb(f"pull{t}", [P, S], F32, {2: "dk_code", 3: "relay"}.get(t)))
+            nc.vector.tensor_tensor(pull[t][:], y_got[t][:], y_win[t][:], ALU.subtract)
 
-        h_bank = [psum.tile([P, S], F32, name=f"h_bank{t}", tag=f"bank{t}") for t in range(PACK)]
-        h_win = [sb(f"h_win{t}", [P, S], F32) for t in range(PACK)]
-        g_win = [sb(f"g_win{t}", [P, S], F32) for t in range(PACK)]
+        z_planes = [sb(f"z_planes{h}", [P, PACK, HALF], BF16) for h in range(2)]
+        units = [(t, (h,)) for h in range(2) for t in range(PACK)]
+        final = len(units) - 1
 
-        def interleave(dst, planes):
-            nc.vector.tensor_copy(
-                dst.rearrange("p (c i t) -> p c t i", i=4, t=PACK),
-                planes.rearrange("p t (c i) -> p c t i", i=4),
-            )
+        def by_halves(ap, hs):
+            return ap.rearrange("p (h c) -> p h c", h=len(hs))
 
-        ring = []
-
-        def ring_tag():
-            ring.append(len(ring))
-            return f"ring{ring[-1] % RING}"
-
-        def empty_h(h):
-            for t in range(PACK):
-                nc.vector.tensor_copy(h_win[t][:, halves[h]], h_bank[t][:, halves[h]])
-                nc.scalar.activation(g_win[t][:, halves[h]], h_bank[t][:, halves[h]], ACT.Tanh, scale=0.5)
-
-        for h in range(2):
-            cols = halves[h]
-            if h == 1:
-                empty_h(0)
-            z_planes = sb(f"z_planes{h}", [P, PACK, HALF], BF16)
-            gate = []
-            for t in range(PACK + 1):
-                if t < PACK:
-                    d_got = fetch(f"d_got{h}{t}", d_win[t], n2_t[:, lcols[h]], ring_tag())
-                    gap = sb(f"gap{h}{t}", [P, HALF], F32)
-                    nc.vector.tensor_tensor(gap[:], d_got[:], d_win[t][:, cols], ALU.subtract)
-                if t > 0:
-                    u = t - 1
-                    step = sb(f"step{h}{u}", [P, HALF], F32)
-                    nc.vector.scalar_tensor_tensor(step[:], gate[u][:], 1.0, pull[u][:, cols], ALU.add, ALU.mult)
-                    nc.vector.scalar_tensor_tensor(z_planes[:, u, :], step[:], 0.5, y_win[u][:, cols], ALU.mult, ALU.add)
-                if t < PACK:
-                    gate.append(sb(f"gate{h}{t}", [P, HALF], F32))
-                    nc.scalar.activation(gate[t][:], gap[:], ACT.Tanh, scale=0.03125)
+        def second_product(h):
             z_grouped = sb(f"z_grouped{h}", [P, PACK * HALF], BF16)
-            interleave(z_grouped[:], z_planes[:])
+            nc.vector.tensor_copy(
+                z_grouped[:].rearrange("p (c i t) -> p c t i", i=4, t=PACK),
+                z_planes[h][:].rearrange("p t (c i) -> p c t i", i=4),
+            )
             z_code = sb(f"z_code{h}", [P, HALF], U32)
             z_scale = sb(f"z_scale{h}", [P, HALF], U8)
             nc.vector.quantize_mx(out=z_code[:].bitcast(FP8X4), scales=z_scale[:], in_=z_grouped[:])
             for t in range(PACK):
-                product(h_bank[t], cols, fp4_slice(w2_code, t), w2_scale[:, P * t : P * (t + 1)], z_code[:], z_scale[:])
-        empty_h(1)
+                product(h_bank[t], halves[h], fp4_slice(w2_code, t), w2_scale[:, P * t : P * (t + 1)], z_code[:], z_scale[:])
+
+        gate = []
+        for k in range(len(units) + 1):
+            if k < len(units):
+                t, hs = units[k]
+                cols = slice(HALF * hs[0], HALF * (hs[-1] + 1))
+                if t == len(d_win):
+                    d_win.append(sb(f"d_win{t}", [P, S], F32, "gap0"))
+                    nc.scalar.copy(d_win[t][:], d_bank[t][:])
+                d_got = sb(f"d_got{k}", [P, HALF * len(hs)], F32, f"ring{k % RING}")
+                for i, h in enumerate(hs):
+                    nc.scalar.activation(d_got[:, halves[i]], d_win[t][:].indirect(n2_t[:, lcols[h]]), ACT.Copy)
+                gap = sb(f"gap{k}", [P, HALF * len(hs)], F32)
+                nc.vector.tensor_tensor(gap[:], d_got[:], d_win[t][:, cols], ALU.subtract)
+            if k > 0:
+                u, us = units[k - 1]
+                ucols = slice(HALF * us[0], HALF * (us[-1] + 1))
+                step = sb(f"step{k - 1}", [P, HALF * len(us)], F32)
+                nc.vector.scalar_tensor_tensor(step[:], gate[k - 1][:], 1.0, pull[u][:, ucols], ALU.add, ALU.mult)
+                nc.vector.scalar_tensor_tensor(
+                    z_planes[us[0]][:, u, :], step[:], 0.5, y_win[u][:, ucols], ALU.mult, ALU.add
+                )
+                if (u, us) == (last, (0,)):
+                    second_product(0)
+            if k < len(units):
+                gate.append(sb(f"gate{k}", [P, HALF * len(hs)], F32))
+                nc.scalar.activation(gate[k][:], gap[:], ACT.Tanh, scale=0.03125)
+
+        late = [f"gap{final}", "gap0", f"ring{final % RING}", f"gate{final}"]
+        g_win = [sb(f"g_win{t}", [P, S], F32, late[t]) for t in range(PACK)]
+        h_win = [sb(f"h_win{t}", [P, S], F32, f"y_win{t}") for t in range(PACK)]
+        for t in range(PACK):
+            nc.scalar.activation(g_win[t][:, halves[0]], h_bank[t][:, halves[0]], ACT.Tanh, scale=0.5)
+            nc.scalar.copy(h_win[t][:, halves[0]], h_bank[t][:, halves[0]])
+        second_product(1)
+        for t in range(PACK):
+            nc.scalar.activation(g_win[t][:, halves[1]], h_bank[t][:, halves[1]], ACT.Tanh, scale=0.5)
+            nc.vector.tensor_copy(h_win[t][:, halves[1]], h_bank[t][:, halves[1]])
+
+        new = []
+        for t in range(PACK):
+            old = sb(f"old{t}", [P, W], F32)
+            nc.scalar.activation(old[:], h_win[t][:].indirect(n3_t[:]), ACT.Copy, scale=0.5)
+            g_got = sb(f"g_got{t}", [P, W], F32)
+            nc.vector.tensor_copy(g_got[:], g_win[t][:].indirect(n4_t[:]))
+            new.append(sb(f"new{t}", [P, W], F32))
+            nc.vector.scalar_tensor_tensor(new[t][:], g_got[:], 1.0, old[:], ALU.add, ALU.mult)
 
         out_rows = out_0.rearrange("(p t) c -> p t c", t=PACK)
         o_grouped = [sb(f"o_grouped{h}", [P, PACK * HALF], BF16) for h in range(2)]
-        new = []
-        for t in range(PACK + 1):
-            if t < PACK:
-                old = sb(f"old{t}", [P, W], F32)
-                nc.scalar.activation(old[:], h_win[t][:].indirect(n3_t[:]), ACT.Copy, scale=0.5)
-                g_got = sb(f"g_got{t}", [P, W], F32)
-                nc.vector.tensor_copy(g_got[:], g_win[t][:].indirect(n4_t[:]))
-                ra = sb(f"ra{t}", [P, W], F32)
-                nc.vector.scalar_tensor_tensor(ra[:], g_got[:], 1.0, old[:], ALU.add, ALU.mult)
-                new.append(ra)
-            if t > 0:
-                u = t - 1
-                nc.scalar.activation(h_win[u][:].indirect(n3_t[:]), new[u][:], ACT.Copy)
-                nc.sync.dma_start(out_rows[:, u, :], h_win[u][:])
-                for h in range(2):
-                    nc.vector.tensor_copy(o_grouped[h][:, u : PACK * HALF : PACK], h_win[u][:, halves[h]])
+        for t in range(PACK):
+            nc.scalar.activation(h_win[t][:].indirect(n3_t[:]), new[t][:], ACT.Copy)
+            nc.sync.dma_start(out_rows[:, t, :], h_win[t][:])
+            for h in range(2):
+                nc.vector.tensor_copy(o_grouped[h][:, t : PACK * HALF : PACK], h_win[t][:, halves[h]])
 
         o_code = sb("o_code", [P, S], U32)
         o_scale = sb("o_scale", [P, S], U8)

@@ -15,12 +15,14 @@ ALU = mybir.AluOpType
 
 P = 128
 PACK = 4
-T = 2048
+QUADS = 4
+GROUP = 16
+TABLE = 2048
 S = 512
 W = 384
 HALF = S // 2
-RING = 3
-V_EMPTIES = 3
+RING = 2
+V_PULLS = 2
 FLOPS = 3 * 2 * 512 * 512 * 512
 
 
@@ -29,6 +31,10 @@ def tile_picked_twkeypullbkgate_none_po_kernel(
     offs, k1, two, n1, n2, n3, n4, out_0, out_1, out_2,
 ):
     nc = tc.nc
+    halves = [slice(HALF * h, HALF * (h + 1)) for h in range(2)]
+    list_halves = [slice(HALF // GROUP * h, HALF // GROUP * (h + 1)) for h in range(2)]
+    last = PACK - 1
+
     with ExitStack() as ctx:
         keep = ctx.enter_context(tc.tile_pool(name="keep", bufs=1))
         psum = ctx.enter_context(tc.psum_pool(name="psum", bufs=1))
@@ -42,39 +48,53 @@ def tile_picked_twkeypullbkgate_none_po_kernel(
             return tile
 
         def load_scale_rows(queue, plane, scales):
-            for q in range(4):
+            for q in range(QUADS):
                 queue.dma_start(plane[32 * q : 32 * q + 4, :].bitcast(I32), scales[0, 4 * q : 4 * q + 4, :].bitcast(I32))
 
         def words_view(ap):
             return ap[0].rearrange("p n t -> p (n t)").bitcast(I32)
 
-        x_plane = sb("x_plane", [P, T], U8)
-        d_plane = sb("d_plane", [P, T], U8)
-        w1_plane = sb("w1_plane", [P, S], U8, "relay")
+        def deal(engine_copy, dst, src):
+            engine_copy(dst.rearrange("p (t m) -> p t m", t=PACK), src.rearrange("p (m t) -> p t m", t=PACK))
+
+        def gather_packed(name, window, offsets, dtype, tag=None):
+            picked = sb(name, [P, GROUP * offsets.shape[1]], dtype, tag)
+            nc.vector.tensor_copy(picked[:], window[:].indirect(offsets))
+            return picked
+
+        def product(out, lhs, lhs_scale, rhs, rhs_scale):
+            nc.tensor.matmul_mx(out=out, lhsT=lhs, lhsT_scale=lhs_scale, rhs=rhs.bitcast(FP8X4), rhs_scale=rhs_scale, start=True, stop=True)
+
+        def fp4_slice(code, t):
+            return code[:, 2 * P * t : 2 * P * (t + 1)].bitcast(FP4X4)
+
+        def col_slice(tile, t):
+            return tile[:, P * t : P * (t + 1)]
+
+        x_plane = sb("x_plane", [P, TABLE], U8)
+        d_plane = sb("d_plane", [P, TABLE], U8)
+        w1_plane = sb("w1_plane", [P, S], U8)
         w2_plane = sb("w2_plane", [P, S], U8)
         dk_plane = sb("dk_plane", [P, S], U8)
-        nc.vector.memset(x_plane[:].bitcast(I32), 0)
-        nc.vector.memset(w1_plane[:].bitcast(I32), 0)
-        nc.vector.memset(d_plane[:].bitcast(I32), 0)
-        nc.vector.memset(w2_plane[:].bitcast(I32), 0)
-        nc.vector.memset(dk_plane[:].bitcast(I32), 0)
+        for plane in (x_plane, w1_plane, d_plane, w2_plane, dk_plane):
+            nc.vector.memset(plane[:].bitcast(I32), 0)
 
         offs_t = load_list("offs_t", offs)
         w1_raw = sb("w1_raw", [P, 2 * S], U8)
         nc.sync.dma_start(w1_raw[:].bitcast(I32), w1_words[0].bitcast(I32))
         load_scale_rows(nc.sync, x_plane, x_scales)
         two_t = load_list("two_t", two)
-        x_tab = sb("x_tab", [P, T], U32)
+        x_tab = sb("x_tab", [P, TABLE], U32)
         nc.sync.dma_start(x_tab[:].bitcast(I32), words_view(x_words))
         load_scale_rows(nc.sync, w1_plane, w1_scales)
         w2_raw = sb("w2_raw", [P, 2 * S], U8)
         nc.gpsimd.dma_start(w2_raw[:].bitcast(I32), w2_words[0].bitcast(I32))
         for a in range(2):
-            nc.gpsimd.dma_start(d_plane[a:P:16, :].bitcast(I32), d_scales[0, a:16:2, :].bitcast(I32))
+            nc.gpsimd.dma_start(d_plane[a:P:GROUP, :].bitcast(I32), d_scales[0, a:16:2, :].bitcast(I32))
         k1_t = load_list("k1_t", k1)
         gain = sb("gain", [P, PACK], F32)
         nc.sync.dma_start(gain[:], gn.rearrange("(p t) o -> p (t o)", t=PACK))
-        d_tab = sb("d_tab", [P, T], U32)
+        d_tab = sb("d_tab", [P, TABLE], U32)
         nc.sync.dma_start(d_tab[:].bitcast(I32), words_view(d_words))
         n1_t = load_list("n1_t", n1)
         n2_t = load_list("n2_t", n2)
@@ -82,62 +102,36 @@ def tile_picked_twkeypullbkgate_none_po_kernel(
         n3_t = load_list("n3_t", n3)
         n4_t = load_list("n4_t", n4)
 
-        def deal(engine_copy, dst, src):
-            engine_copy(dst.rearrange("p (t m) -> p t m", t=PACK), src.rearrange("p (m t) -> p t m", t=PACK))
-
-        def gather_packed(name, window, offsets, dtype, tag=None):
-            picked = sb(name, [P, S], dtype, tag)
-            nc.vector.tensor_copy(picked[:], window[:].indirect(offsets[:]))
-            return picked
-
-        xo_scale = gather_packed("xo_scale", x_plane, offs_t, U8)
-        xt_scale = gather_packed("xt_scale", x_plane, two_t, U8)
-        xo_code = gather_packed("xo_code", x_tab, offs_t, U32)
+        xo_scale = gather_packed("xo_scale", x_plane, offs_t[:], U8)
+        xt_scale = gather_packed("xt_scale", x_plane, two_t[:], U8)
+        xo_code = [gather_packed("xo_code0", x_tab, offs_t[:, list_halves[0]], U32)]
         w1_code = sb("w1_code", [P, 2 * S], U8)
         w1_scale = sb("w1_scale", [P, S], U8)
         deal(nc.scalar.copy, w1_code[:].bitcast(U16), w1_raw[:].bitcast(U16))
         deal(nc.vector.tensor_copy, w1_scale[:], w1_plane[:])
+        xo_code.append(gather_packed("xo_code1", x_tab, offs_t[:, list_halves[1]], U32, "w1_plane"))
 
-        dk_bytes = gather_packed("dk_bytes", d_plane, k1_t, U8, "relay")
+        dk_bytes = gather_packed("dk_bytes", d_plane, k1_t[:], U8)
         dk_dealt = sb("dk_dealt", [P, S], U8)
         deal(nc.vector.tensor_copy, dk_dealt[:], dk_bytes[:])
         for a in range(4):
-            src_row = 16 * (a // 2) + a % 2
+            src_row = GROUP * (a // 2) + a % 2
             nc.sync.dma_start(dk_plane[a:P:32, :].bitcast(I32), dk_dealt[src_row:P:32, :].bitcast(I32))
 
-        def product(bank, cols, lhs, lhs_scale, rhs, rhs_scale):
-            nc.tensor.matmul_mx(out=bank[:, cols], lhsT=lhs, lhsT_scale=lhs_scale, rhs=rhs.bitcast(FP8X4), rhs_scale=rhs_scale, start=True, stop=True)
-
-        def fp4_slice(code, t):
-            return code[:, 2 * P * t : 2 * P * (t + 1)].bitcast(FP4X4)
-
-        whole = slice(0, S)
-        halves = [slice(HALF * h, HALF * (h + 1)) for h in range(2)]
-        lcols = [slice(HALF // 16 * h, HALF // 16 * (h + 1)) for h in range(2)]
-
-        y_win = []
-        for t in range(PACK):
-            bank = psum.tile([P, S], F32, name=f"y_bank{t}", tag=f"bank{t}")
-            product(bank, whole, fp4_slice(w1_code, t), w1_scale[:, P * t : P * (t + 1)], xo_code[:], xo_scale[:])
-            win = sb(f"y_win{t}", [P, S], F32)
-            nc.scalar.activation(win[:], bank[:], ACT.Copy, scale=gain[:, t : t + 1])
-            y_win.append(win)
-
-        def fetch(name, window, offsets, tag=None):
-            got = sb(name, [P, HALF], F32, tag)
-            nc.scalar.activation(got[:], window[:].indirect(offsets), ACT.Copy)
-            return got
-
-        last = PACK - 1
+        y_bank = [psum.tile([P, S], F32, name=f"y_bank{t}", tag=f"bank{t}") for t in range(PACK)]
+        y_win = [sb(f"y_win{t}", [P, S], F32) for t in range(PACK)]
+        for h in range(2):
+            for t in range(PACK):
+                product(y_bank[t][:, halves[h]], fp4_slice(w1_code, t), col_slice(w1_scale, t), xo_code[h][:], xo_scale[:, halves[h]])
+                nc.scalar.activation(y_win[t][:, halves[h]], y_bank[t][:, halves[h]], ACT.Copy, scale=gain[:, t : t + 1])
         y_got = []
         for t in range(PACK):
-            got = sb(f"y_got{t}", [P, S], F32)
+            y_got.append(sb(f"y_got{t}", [P, S], F32))
             for h in range(2):
-                nc.scalar.activation(got[:, halves[h]], y_win[t][:].indirect(n1_t[:, lcols[h]]), ACT.Copy)
-            y_got.append(got)
+                nc.scalar.activation(y_got[t][:, halves[h]], y_win[t][:].indirect(n1_t[:, list_halves[h]]), ACT.Copy)
 
-        xt_code = gather_packed("xt_code", x_tab, two_t, U32, "relay")
-        dk_words = gather_packed("dk_words", d_tab, k1_t, U32)
+        xt_code = gather_packed("xt_code", x_tab, two_t[:], U32, "dk_bytes")
+        dk_words = gather_packed("dk_words", d_tab, k1_t[:], U32)
         dk_code = sb("dk_code", [P, S], U32)
         nc.vector.tensor_copy(dk_code[:].rearrange("p (t m) -> p m t", t=PACK), dk_words[:].rearrange("p (m t) -> p m t", t=PACK))
 
@@ -149,65 +143,53 @@ def tile_picked_twkeypullbkgate_none_po_kernel(
         d_bank = []
         for t in range(PACK):
             d_bank.append(psum.tile([P, S], F32, name=f"d_bank{t}", tag=f"bank{PACK + t}"))
-            product(d_bank[t], whole, dk_code[:, P * t : P * (t + 1)].bitcast(FP8X4), dk_plane[:, P * t : P * (t + 1)], xt_code[:], xt_scale[:])
-        d_win = [sb(f"d_win{t}", [P, S], F32) for t in range(V_EMPTIES)]
+            product(d_bank[t][:], col_slice(dk_code, t).bitcast(FP8X4), col_slice(dk_plane, t), xt_code[:], xt_scale[:])
+        d_win = [sb(f"d_win{t}", [P, S], F32) for t in range(PACK)]
         h_bank = [psum.tile([P, S], F32, name=f"h_bank{t}", tag=f"bank{t}") for t in range(PACK)]
-
         pull = []
         for t in range(PACK):
-            if t < V_EMPTIES:
-                nc.vector.tensor_copy(d_win[t][:], d_bank[t][:])
-            pull.append(sb(f"pull{t}", [P, S], F32, {2: "dk_code", 3: "relay"}.get(t)))
-            nc.vector.tensor_tensor(pull[t][:], y_got[t][:], y_win[t][:], ALU.subtract)
+            nc.vector.tensor_copy(d_win[t][:], d_bank[t][:])
+            pull.append(sb(f"pull{t}", [P, S], F32))
+            engine = nc.vector if t < V_PULLS else nc.gpsimd
+            engine.tensor_tensor(pull[t][:], y_got[t][:], y_win[t][:], ALU.subtract)
 
-        z_planes = [sb(f"z_planes{h}", [P, PACK, HALF], BF16) for h in range(2)]
-        units = [(t, (h,)) for h in range(2) for t in range(PACK)]
-        final = len(units) - 1
-
-        def by_halves(ap, hs):
-            return ap.rearrange("p (h c) -> p h c", h=len(hs))
+        z_rows = [sb(f"z_rows{h}", [P, PACK, HALF], BF16) for h in range(2)]
 
         def second_product(h):
             z_grouped = sb(f"z_grouped{h}", [P, PACK * HALF], BF16)
             nc.vector.tensor_copy(
                 z_grouped[:].rearrange("p (c i t) -> p c t i", i=4, t=PACK),
-                z_planes[h][:].rearrange("p t (c i) -> p c t i", i=4),
+                z_rows[h][:].rearrange("p t (c i) -> p c t i", i=4),
             )
             z_code = sb(f"z_code{h}", [P, HALF], U32)
             z_scale = sb(f"z_scale{h}", [P, HALF], U8)
             nc.vector.quantize_mx(out=z_code[:].bitcast(FP8X4), scales=z_scale[:], in_=z_grouped[:])
             for t in range(PACK):
-                product(h_bank[t], halves[h], fp4_slice(w2_code, t), w2_scale[:, P * t : P * (t + 1)], z_code[:], z_scale[:])
+                product(h_bank[t][:, halves[h]], fp4_slice(w2_code, t), col_slice(w2_scale, t), z_code[:], z_scale[:])
 
+        pieces = [(h, t) for h in range(2) for t in range(PACK)]
+        final = len(pieces) - 1
         gate = []
-        for k in range(len(units) + 1):
-            if k < len(units):
-                t, hs = units[k]
-                cols = slice(HALF * hs[0], HALF * (hs[-1] + 1))
-                if t == len(d_win):
-                    d_win.append(sb(f"d_win{t}", [P, S], F32, "gap0"))
-                    nc.scalar.copy(d_win[t][:], d_bank[t][:])
-                d_got = sb(f"d_got{k}", [P, HALF * len(hs)], F32, f"ring{k % RING}")
-                for i, h in enumerate(hs):
-                    nc.scalar.activation(d_got[:, halves[i]], d_win[t][:].indirect(n2_t[:, lcols[h]]), ACT.Copy)
-                gap = sb(f"gap{k}", [P, HALF * len(hs)], F32)
-                nc.vector.tensor_tensor(gap[:], d_got[:], d_win[t][:, cols], ALU.subtract)
+        for k in range(len(pieces) + 1):
+            if k <= final:
+                h, t = pieces[k]
+                d_got = sb(f"d_got{k}", [P, HALF], F32, f"ring{k % RING}")
+                nc.scalar.activation(d_got[:], d_win[t][:].indirect(n2_t[:, list_halves[h]]), ACT.Copy)
+                gap = sb(f"gap{k}", [P, HALF], F32)
+                nc.vector.tensor_tensor(gap[:], d_got[:], d_win[t][:, halves[h]], ALU.subtract)
             if k > 0:
-                u, us = units[k - 1]
-                ucols = slice(HALF * us[0], HALF * (us[-1] + 1))
-                step = sb(f"step{k - 1}", [P, HALF * len(us)], F32)
-                nc.vector.scalar_tensor_tensor(step[:], gate[k - 1][:], 1.0, pull[u][:, ucols], ALU.add, ALU.mult)
-                nc.vector.scalar_tensor_tensor(
-                    z_planes[us[0]][:, u, :], step[:], 0.5, y_win[u][:, ucols], ALU.mult, ALU.add
-                )
-                if (u, us) == (last, (0,)):
+                h_prev, t_prev = pieces[k - 1]
+                step = sb(f"step{k - 1}", [P, HALF], F32)
+                nc.vector.scalar_tensor_tensor(step[:], gate[k - 1][:], 1.0, pull[t_prev][:, halves[h_prev]], ALU.add, ALU.mult)
+                nc.vector.scalar_tensor_tensor(z_rows[h_prev][:, t_prev, :], step[:], 0.5, y_win[t_prev][:, halves[h_prev]], ALU.mult, ALU.add)
+                if (h_prev, t_prev) == (0, last):
                     second_product(0)
-            if k < len(units):
-                gate.append(sb(f"gate{k}", [P, HALF * len(hs)], F32))
-                nc.scalar.activation(gate[k][:], gap[:], ACT.Tanh, scale=0.03125)
+            if k <= final:
+                gate.append(sb(f"gate{k}", [P, HALF], F32))
+                nc.scalar.activation(gate[k][:], gap[:], ACT.Tanh, scale=0.0625 / 2)
 
-        late = [f"gap{final}", "gap0", f"ring{final % RING}", f"gate{final}"]
-        g_win = [sb(f"g_win{t}", [P, S], F32, late[t]) for t in range(PACK)]
+        last_piece_tags = [f"gap{final}", f"d_win{last}", f"ring{final % RING}", f"gate{final}"]
+        g_win = [sb(f"g_win{t}", [P, S], F32, last_piece_tags[t]) for t in range(PACK)]
         h_win = [sb(f"h_win{t}", [P, S], F32, f"y_win{t}") for t in range(PACK)]
         for t in range(PACK):
             nc.scalar.activation(g_win[t][:, halves[0]], h_bank[t][:, halves[0]], ACT.Tanh, scale=0.5)
@@ -217,19 +199,19 @@ def tile_picked_twkeypullbkgate_none_po_kernel(
             nc.scalar.activation(g_win[t][:, halves[1]], h_bank[t][:, halves[1]], ACT.Tanh, scale=0.5)
             nc.vector.tensor_copy(h_win[t][:, halves[1]], h_bank[t][:, halves[1]])
 
-        new = []
+        ra = []
         for t in range(PACK):
-            old = sb(f"old{t}", [P, W], F32)
-            nc.scalar.activation(old[:], h_win[t][:].indirect(n3_t[:]), ACT.Copy, scale=0.5)
+            old_half = sb(f"old_half{t}", [P, W], F32)
+            nc.scalar.activation(old_half[:], h_win[t][:].indirect(n3_t[:]), ACT.Copy, scale=0.5)
             g_got = sb(f"g_got{t}", [P, W], F32)
             nc.vector.tensor_copy(g_got[:], g_win[t][:].indirect(n4_t[:]))
-            new.append(sb(f"new{t}", [P, W], F32))
-            nc.vector.scalar_tensor_tensor(new[t][:], g_got[:], 1.0, old[:], ALU.add, ALU.mult)
+            ra.append(sb(f"ra{t}", [P, W], F32))
+            nc.vector.scalar_tensor_tensor(ra[t][:], g_got[:], 1.0, old_half[:], ALU.add, ALU.mult)
 
         out_rows = out_0.rearrange("(p t) c -> p t c", t=PACK)
         o_grouped = [sb(f"o_grouped{h}", [P, PACK * HALF], BF16) for h in range(2)]
         for t in range(PACK):
-            nc.scalar.activation(h_win[t][:].indirect(n3_t[:]), new[t][:], ACT.Copy)
+            nc.scalar.activation(h_win[t][:].indirect(n3_t[:]), ra[t][:], ACT.Copy)
             nc.sync.dma_start(out_rows[:, t, :], h_win[t][:])
             for h in range(2):
                 nc.vector.tensor_copy(o_grouped[h][:, t : PACK * HALF : PACK], h_win[t][:, halves[h]])
@@ -239,5 +221,5 @@ def tile_picked_twkeypullbkgate_none_po_kernel(
         for h in range(2):
             nc.vector.quantize_mx(out=o_code[:, halves[h]].bitcast(FP8X4), scales=o_scale[:, halves[h]], in_=o_grouped[h][:])
             nc.sync.dma_start(words_view(out_1)[:, halves[h]], o_code[:, halves[h]].bitcast(I32))
-        for q in range(4):
+        for q in range(QUADS):
             nc.scalar.dma_start(out_2[0, 4 * q : 4 * q + 4, :].bitcast(I32), o_scale[32 * q : 32 * q + 4, :].bitcast(I32))

from contextlib import ExitStack

import concourse.mybir as mybir

F32 = mybir.dt.float32
BF16 = mybir.dt.bfloat16
I32 = mybir.dt.int32
U32 = mybir.dt.uint32
U16 = mybir.dt.uint16
U8 = mybir.dt.uint8
FP8X4 = mybir.dt.float8_e4m3fn_x4
FP4X4 = mybir.dt.float4_e2m1fn_x4
ACT = mybir.ActivationFunctionType
ALU = mybir.AluOpType

P = 128
PACK = 4
QUADS = 4
GROUP = 16
TABLE = 2048
S = 512
W = 384
HALF = S // 2
RING = 2
V_PULLS = 2
FLOPS = 3 * 2 * 512 * 512 * 512


def tile_picked_twkeypullbkgate_none_po_kernel(
    tc, x_words, x_scales, w1_words, w1_scales, d_words, d_scales, gn, w2_words, w2_scales,
    offs, k1, two, n1, n2, n3, n4, out_0, out_1, out_2,
):
    nc = tc.nc
    halves = [slice(HALF * h, HALF * (h + 1)) for h in range(2)]
    list_halves = [slice(HALF // GROUP * h, HALF // GROUP * (h + 1)) for h in range(2)]
    last = PACK - 1

    with ExitStack() as ctx:
        keep = ctx.enter_context(tc.tile_pool(name="keep", bufs=1))
        psum = ctx.enter_context(tc.psum_pool(name="psum", bufs=1))

        def sb(name, shape, dtype, tag=None):
            return keep.tile(shape, dtype, name=name, tag=tag or name, align_bytes=64)

        def load_list(name, src):
            tile = sb(name, list(src.shape), U16)
            nc.sync.dma_start(tile[:], src)
            return tile

        def load_scale_rows(queue, plane, scales):
            for q in range(QUADS):
                queue.dma_start(plane[32 * q : 32 * q + 4, :].bitcast(I32), scales[0, 4 * q : 4 * q + 4, :].bitcast(I32))

        def words_view(ap):
            return ap[0].rearrange("p n t -> p (n t)").bitcast(I32)

        def deal(engine_copy, dst, src):
            engine_copy(dst.rearrange("p (t m) -> p t m", t=PACK), src.rearrange("p (m t) -> p t m", t=PACK))

        def gather_packed(name, window, offsets, dtype, tag=None):
            picked = sb(name, [P, GROUP * offsets.shape[1]], dtype, tag)
            nc.vector.tensor_copy(picked[:], window[:].indirect(offsets))
            return picked

        def product(out, lhs, lhs_scale, rhs, rhs_scale):
            nc.tensor.matmul_mx(out=out, lhsT=lhs, lhsT_scale=lhs_scale, rhs=rhs.bitcast(FP8X4), rhs_scale=rhs_scale, start=True, stop=True)

        def fp4_slice(code, t):
            return code[:, 2 * P * t : 2 * P * (t + 1)].bitcast(FP4X4)

        def col_slice(tile, t):
            return tile[:, P * t : P * (t + 1)]

        x_plane = sb("x_plane", [P, TABLE], U8)
        d_plane = sb("d_plane", [P, TABLE], U8)
        w1_plane = sb("w1_plane", [P, S], U8)
        w2_plane = sb("w2_plane", [P, S], U8)
        dk_plane = sb("dk_plane", [P, S], U8)
        for plane in (x_plane, w1_plane, d_plane, w2_plane, dk_plane):
            nc.vector.memset(plane[:].bitcast(I32), 0)

        offs_t = load_list("offs_t", offs)
        w1_raw = sb("w1_raw", [P, 2 * S], U8)
        nc.sync.dma_start(w1_raw[:].bitcast(I32), w1_words[0].bitcast(I32))
        load_scale_rows(nc.sync, x_plane, x_scales)
        two_t = load_list("two_t", two)
        x_tab = sb("x_tab", [P, TABLE], U32)
        nc.sync.dma_start(x_tab[:].bitcast(I32), words_view(x_words))
        load_scale_rows(nc.sync, w1_plane, w1_scales)
        w2_raw = sb("w2_raw", [P, 2 * S], U8)
        nc.gpsimd.dma_start(w2_raw[:].bitcast(I32), w2_words[0].bitcast(I32))
        for a in range(2):
            nc.gpsimd.dma_start(d_plane[a:P:GROUP, :].bitcast(I32), d_scales[0, a:16:2, :].bitcast(I32))
        k1_t = load_list("k1_t", k1)
        gain = sb("gain", [P, PACK], F32)
        nc.sync.dma_start(gain[:], gn.rearrange("(p t) o -> p (t o)", t=PACK))
        d_tab = sb("d_tab", [P, TABLE], U32)
        nc.sync.dma_start(d_tab[:].bitcast(I32), words_view(d_words))
        n1_t = load_list("n1_t", n1)
        n2_t = load_list("n2_t", n2)
        load_scale_rows(nc.gpsimd, w2_plane, w2_scales)
        n3_t = load_list("n3_t", n3)
        n4_t = load_list("n4_t", n4)

        xo_scale = gather_packed("xo_scale", x_plane, offs_t[:], U8)
        xt_scale = gather_packed("xt_scale", x_plane, two_t[:], U8)
        xo_code = [gather_packed("xo_code0", x_tab, offs_t[:, list_halves[0]], U32)]
        w1_code = sb("w1_code", [P, 2 * S], U8)
        w1_scale = sb("w1_scale", [P, S], U8)
        deal(nc.scalar.copy, w1_code[:].bitcast(U16), w1_raw[:].bitcast(U16))
        deal(nc.vector.tensor_copy, w1_scale[:], w1_plane[:])
        xo_code.append(gather_packed("xo_code1", x_tab, offs_t[:, list_halves[1]], U32, "w1_plane"))

        dk_bytes = gather_packed("dk_bytes", d_plane, k1_t[:], U8)
        dk_dealt = sb("dk_dealt", [P, S], U8)
        deal(nc.vector.tensor_copy, dk_dealt[:], dk_bytes[:])
        for a in range(4):
            src_row = GROUP * (a // 2) + a % 2
            nc.sync.dma_start(dk_plane[a:P:32, :].bitcast(I32), dk_dealt[src_row:P:32, :].bitcast(I32))

        y_bank = [psum.tile([P, S], F32, name=f"y_bank{t}", tag=f"bank{t}") for t in range(PACK)]
        y_win = [sb(f"y_win{t}", [P, S], F32) for t in range(PACK)]
        for h in range(2):
            for t in range(PACK):
                product(y_bank[t][:, halves[h]], fp4_slice(w1_code, t), col_slice(w1_scale, t), xo_code[h][:], xo_scale[:, halves[h]])
                nc.scalar.activation(y_win[t][:, halves[h]], y_bank[t][:, halves[h]], ACT.Copy, scale=gain[:, t : t + 1])
        y_got = []
        for t in range(PACK):
            y_got.append(sb(f"y_got{t}", [P, S], F32))
            for h in range(2):
                nc.scalar.activation(y_got[t][:, halves[h]], y_win[t][:].indirect(n1_t[:, list_halves[h]]), ACT.Copy)

        xt_code = gather_packed("xt_code", x_tab, two_t[:], U32, "dk_bytes")
        dk_words = gather_packed("dk_words", d_tab, k1_t[:], U32)
        dk_code = sb("dk_code", [P, S], U32)
        nc.vector.tensor_copy(dk_code[:].rearrange("p (t m) -> p m t", t=PACK), dk_words[:].rearrange("p (m t) -> p m t", t=PACK))

        w2_code = sb("w2_code", [P, 2 * S], U8)
        w2_scale = sb("w2_scale", [P, S], U8)
        deal(nc.scalar.copy, w2_code[:].bitcast(U16), w2_raw[:].bitcast(U16))
        deal(nc.gpsimd.tensor_copy, w2_scale[:], w2_plane[:])

        d_bank = []
        for t in range(PACK):
            d_bank.append(psum.tile([P, S], F32, name=f"d_bank{t}", tag=f"bank{PACK + t}"))
            product(d_bank[t][:], col_slice(dk_code, t).bitcast(FP8X4), col_slice(dk_plane, t), xt_code[:], xt_scale[:])
        d_win = [sb(f"d_win{t}", [P, S], F32) for t in range(PACK)]
        h_bank = [psum.tile([P, S], F32, name=f"h_bank{t}", tag=f"bank{t}") for t in range(PACK)]
        pull = []
        for t in range(PACK):
            nc.vector.tensor_copy(d_win[t][:], d_bank[t][:])
            pull.append(sb(f"pull{t}", [P, S], F32))
            engine = nc.vector if t < V_PULLS else nc.gpsimd
            engine.tensor_tensor(pull[t][:], y_got[t][:], y_win[t][:], ALU.subtract)

        z_rows = [sb(f"z_rows{h}", [P, PACK, HALF], BF16) for h in range(2)]

        def second_product(h):
            z_grouped = sb(f"z_grouped{h}", [P, PACK * HALF], BF16)
            nc.vector.tensor_copy(
                z_grouped[:].rearrange("p (c i t) -> p c t i", i=4, t=PACK),
                z_rows[h][:].rearrange("p t (c i) -> p c t i", i=4),
            )
            z_code = sb(f"z_code{h}", [P, HALF], U32)
            z_scale = sb(f"z_scale{h}", [P, HALF], U8)
            nc.vector.quantize_mx(out=z_code[:].bitcast(FP8X4), scales=z_scale[:], in_=z_grouped[:])
            for t in range(PACK):
                product(h_bank[t][:, halves[h]], fp4_slice(w2_code, t), col_slice(w2_scale, t), z_code[:], z_scale[:])

        pieces = [(h, t) for h in range(2) for t in range(PACK)]
        final = len(pieces) - 1
        gate = []
        for k in range(len(pieces) + 1):
            if k <= final:
                h, t = pieces[k]
                d_got = sb(f"d_got{k}", [P, HALF], F32, f"ring{k % RING}")
                nc.scalar.activation(d_got[:], d_win[t][:].indirect(n2_t[:, list_halves[h]]), ACT.Copy)
                gap = sb(f"gap{k}", [P, HALF], F32)
                nc.vector.tensor_tensor(gap[:], d_got[:], d_win[t][:, halves[h]], ALU.subtract)
            if k > 0:
                h_prev, t_prev = pieces[k - 1]
                step = sb(f"step{k - 1}", [P, HALF], F32)
                nc.vector.scalar_tensor_tensor(step[:], gate[k - 1][:], 1.0, pull[t_prev][:, halves[h_prev]], ALU.add, ALU.mult)
                nc.vector.scalar_tensor_tensor(z_rows[h_prev][:, t_prev, :], step[:], 0.5, y_win[t_prev][:, halves[h_prev]], ALU.mult, ALU.add)
                if (h_prev, t_prev) == (0, last):
                    second_product(0)
            if k <= final:
                gate.append(sb(f"gate{k}", [P, HALF], F32))
                nc.scalar.activation(gate[k][:], gap[:], ACT.Tanh, scale=0.0625 / 2)

        last_piece_tags = [f"gap{final}", f"d_win{last}", f"ring{final % RING}", f"gate{final}"]
        g_win = [sb(f"g_win{t}", [P, S], F32, last_piece_tags[t]) for t in range(PACK)]
        h_win = [sb(f"h_win{t}", [P, S], F32, f"y_win{t}") for t in range(PACK)]
        for t in range(PACK):
            nc.scalar.activation(g_win[t][:, halves[0]], h_bank[t][:, halves[0]], ACT.Tanh, scale=0.5)
            nc.scalar.copy(h_win[t][:, halves[0]], h_bank[t][:, halves[0]])
        second_product(1)
        for t in range(PACK):
            nc.scalar.activation(g_win[t][:, halves[1]], h_bank[t][:, halves[1]], ACT.Tanh, scale=0.5)
            nc.vector.tensor_copy(h_win[t][:, halves[1]], h_bank[t][:, halves[1]])

        ra = []
        for t in range(PACK):
            old_half = sb(f"old_half{t}", [P, W], F32)
            nc.scalar.activation(old_half[:], h_win[t][:].indirect(n3_t[:]), ACT.Copy, scale=0.5)
            g_got = sb(f"g_got{t}", [P, W], F32)
            nc.vector.tensor_copy(g_got[:], g_win[t][:].indirect(n4_t[:]))
            ra.append(sb(f"ra{t}", [P, W], F32))
            nc.vector.scalar_tensor_tensor(ra[t][:], g_got[:], 1.0, old_half[:], ALU.add, ALU.mult)

        out_rows = out_0.rearrange("(p t) c -> p t c", t=PACK)
        o_grouped = [sb(f"o_grouped{h}", [P, PACK * HALF], BF16) for h in range(2)]
        for t in range(PACK):
            nc.scalar.activation(h_win[t][:].indirect(n3_t[:]), ra[t][:], ACT.Copy)
            nc.sync.dma_start(out_rows[:, t, :], h_win[t][:])
            for h in range(2):
                nc.vector.tensor_copy(o_grouped[h][:, t : PACK * HALF : PACK], h_win[t][:, halves[h]])

        o_code = sb("o_code", [P, S], U32)
        o_scale = sb("o_scale", [P, S], U8)
        for h in range(2):
            nc.vector.quantize_mx(out=o_code[:, halves[h]].bitcast(FP8X4), scales=o_scale[:, halves[h]], in_=o_grouped[h][:])
            nc.sync.dma_start(words_view(out_1)[:, halves[h]], o_code[:, halves[h]].bitcast(I32))
        for q in range(QUADS):
            nc.scalar.dma_start(out_2[0, 4 * q : 4 * q + 4, :].bitcast(I32), o_scale[32 * q : 32 * q + 4, :].bitcast(I32))
